import numpy as np
import ml_dtypes


def mxq(x, axis, fmt="e4m3"):
    dtype, down = {"e4m3": (ml_dtypes.float8_e4m3fn, 7), "e5m2": (ml_dtypes.float8_e5m2, 14)}[fmt]
    v = np.moveaxis(np.asarray(x, np.float32).astype(ml_dtypes.bfloat16).astype(np.float64), axis, -1)
    blocks = v.reshape(v.shape[:-1] + (-1, 32))
    amax = np.abs(blocks).max(-1, keepdims=True)
    byte = np.maximum(np.where(amax > 0, np.frexp(amax)[1] - 1 + 127, 0) - down, 1)
    scale = np.exp2(byte - 127.0)
    codes = (blocks / scale).astype(np.float32).astype(dtype).astype(np.float64)
    return np.moveaxis((codes * scale).reshape(v.shape), -1, axis)


WIDE = False


def mx_kscale(k):
    if not WIDE:
        return np.ones(k)
    levels = np.array([10, -10, 5, -5, 0])
    if k % 512:
        return np.exp2(np.random.permutation(np.resize(levels, k // 32))).repeat(32)
    a = np.empty((k // 512, 16))
    for p in range(k // 512):
        a[p, :8] = np.random.permutation(np.resize(levels, 8))
        for g in range(8):
            far = levels[np.abs(levels - a[p, g]) >= 10]
            a[p, g + 8] = far[np.random.randint(len(far))]
    return np.exp2(a.ravel()).repeat(32)


def f64(x):
    return np.asarray(x).astype(np.float64)


def striped(idx):
    return np.tile(idx.reshape(-1, 16).T, (8, 1)).astype(np.uint16)


def unstriped(offs):
    return offs[:16].T.reshape(-1).astype(np.int64)


def pack_weight(w):
    k, n = w.shape
    w = f64(np.asarray(w, np.float32).astype(ml_dtypes.bfloat16)).reshape(k // 32, 32, n)
    amax = np.abs(w).max(1)
    byte = np.clip(np.where(amax > 0, np.frexp(amax)[1] - 1 + 127 - 7, 1), 1, 254)
    scaled = (w * np.exp2(127.0 - byte)[:, None, :]).reshape(k, n).astype(np.float32)
    words = np.ascontiguousarray(scaled.reshape(k // 512, 128, 4, n).transpose(0, 1, 3, 2)).astype(ml_dtypes.float8_e4m3fn).view(np.uint8)
    return words, np.ascontiguousarray(byte.astype(np.uint8).reshape(k // 512, 16, n))


def unpack_weight(words, scales):
    g, p, n, _ = words.shape
    vals = np.ascontiguousarray(words).view(ml_dtypes.float8_e4m3fn).astype(np.float64) * np.repeat(np.exp2(scales.astype(np.float64) - 127.0), 8, axis=1)[..., None]
    return vals.transpose(0, 1, 3, 2).reshape(g * 512, n)


def silu(v):
    return v / (1.0 + np.exp(-np.maximum(v, -700.0)))


K, T, D, S, V, N = 512, 1024, 4, 512, 256, 128


def setup_inputs():
    n = np.random.standard_normal
    s = mx_kscale(K)[:, None]
    words, scales = pack_weight(n((K, N)) / np.sqrt(K) / s)
    return {
        "xT": (n((K, T)) * s).astype(np.float32),
        "w_words": words,
        "w_scales": scales,
        "b": (0.3 * n((N, 1))).astype(np.float32),
        "gate": np.tile(np.random.uniform(0.2, 1.0, (D, 1, V)) / np.sqrt(D), (1, N, 1)).astype(np.float32),
        "offs": striped(np.random.permutation(T)[:S]),
        "pos1": striped(np.random.permutation(S)[:V]),
        "pos2": striped(np.random.permutation(S)[:V]),
        "pos3": striped(np.random.permutation(S)[:V]),
        "pos4": striped(np.random.permutation(S)[:V]),
    }


def reference(xT, w_words, w_scales, b, gate, offs, pos1, pos2, pos3, pos4):
    w = unpack_weight(w_words, w_scales)
    idx = unstriped(offs)
    xq = mxq(f64(xT)[:, idx], 0, "e4m3")
    y = w.T @ xq
    y = silu(y + f64(b))
    return sum(f64(gate[d]) * y[:, unstriped(p)] for d, p in enumerate((pos1, pos2, pos3, pos4)))

@@ -1,0 +1,121 @@
+from contextlib import ExitStack
+
+import concourse.mybir as mybir
+
+K, T, D, S, V, N = 512, 1024, 4, 512, 256, 128
+P = 128
+PACK = 4
+PIECES = ((0, 256), (256, 384), (384, 512))
+LINE = 16
+HALF = V // 2
+
+FLOPS = 2 * K * S * N
+
+F32 = mybir.dt.float32
+BF16 = mybir.dt.bfloat16
+I32 = mybir.dt.int32
+U32 = mybir.dt.uint32
+U16 = mybir.dt.uint16
+U8 = mybir.dt.uint8
+FP8X4 = mybir.dt.float8_e4m3fn_x4
+SILU = mybir.ActivationFunctionType.Silu
+MULT = mybir.AluOpType.mult
+ADD = mybir.AluOpType.add
+
+
+def tile_picked_sub_lin_silu_sub_e_kernel(tc, xT, w_words, w_scales, b, gate, offs, pos1, pos2, pos3, pos4, out):
+    nc = tc.nc
+    with ExitStack() as ctx:
+        keep = ctx.enter_context(tc.tile_pool(name="keep", bufs=1))
+        psum = ctx.enter_context(tc.psum_pool(name="psum", bufs=1))
+
+        offsets = keep.tile([P, S // LINE], U16, name="offsets")
+        places = [keep.tile([P, V // LINE], U16, name=f"places{d}") for d in range(D)]
+        x_rows = [keep.tile([P, T], F32, name=f"x_rows{t}", align_bytes=64) for t in range(PACK)]
+        w_codes = keep.tile([P, N], U32, name="w_codes", align_bytes=64)
+        w_planes = keep.tile([P, N], U8, name="w_planes", align_bytes=64)
+        bias = keep.tile([P, 1], F32, name="bias")
+        gates = keep.tile([P, D, V], F32, name="gates", align_bytes=64)
+        warm = keep.tile([P, 1], F32, name="warm")
+        warm_out = keep.tile([P, 1], F32, name="warm_out")
+
+        nc.vector.memset(warm[:], 0.0)
+        nc.gpsimd.memset(w_planes[:].bitcast(I32), 0)
+        x_view = xT.rearrange("(p t) c -> p t c", t=PACK)
+        nc.scalar.dma_start(x_rows[0][:], x_view[:, 0, :])
+        nc.sync.dma_start(offsets[:], offs)
+        for t in range(1, PACK):
+            nc.sync.dma_start(x_rows[t][:], x_view[:, t, :])
+        nc.scalar.activation(warm_out[:], warm[:], SILU)
+        for q in range(4):
+            (nc.gpsimd if q % 2 else nc.scalar).dma_start(w_planes[32 * q : 32 * q + 4, :].bitcast(I32), w_scales[0, 4 * q : 4 * q + 4, :].bitcast(I32))
+        nc.sync.dma_start(w_codes[:].bitcast(I32), w_words[0].rearrange("p m r -> p (m r)").bitcast(I32))
+        nc.sync.dma_start(bias[:], b)
+        nc.sync.dma_start(gates[:], gate.rearrange("d m v -> m d v"))
+        for d, pos in enumerate((pos1, pos2, pos3, pos4)):
+            nc.sync.dma_start(places[d][:], pos)
+
+        picked = keep.tile([P, PACK, S], F32, name="picked", align_bytes=64)
+        widths = [end - start for start, end in PIECES]
+        grouped = [keep.tile([P, n, PACK], BF16, name=f"grouped{i}", align_bytes=64) for i, n in enumerate(widths)]
+        codes = [keep.tile([P, n], U32, name=f"codes{i}", align_bytes=64) for i, n in enumerate(widths)]
+        planes = [keep.tile([P, n], U8, name=f"planes{i}", align_bytes=64) for i, n in enumerate(widths)]
+        sums = [psum.tile([N, n], F32, name=f"sums{i}") for i, n in enumerate(widths)]
+        y = keep.tile([N, S], F32, name="y", align_bytes=64)
+
+        def cols(i):
+            return slice(*PIECES[i])
+
+        def pair(i, t):
+            source = picked[:, t : t + 2, cols(i)].rearrange("p t c -> p c t")
+            return grouped[i][:, :, t : t + 2], source
+
+        for t in range(PACK - 1):
+            nc.vector.tensor_copy(picked[:, t, :], x_rows[t][:].indirect(offsets[:]))
+            if t == 1:
+                for i in range(3):
+                    nc.scalar.copy(*pair(i, 0))
+        for i, (start, end) in enumerate(PIECES):
+            lines = slice(start // LINE, end // LINE)
+            nc.vector.tensor_copy(picked[:, PACK - 1, cols(i)], x_rows[PACK - 1][:].indirect(offsets[:, lines]))
+        nc.scalar.copy(*pair(0, 2))
+        nc.scalar.copy(*pair(2, 2))
+        nc.vector.tensor_copy(*pair(1, 2))
+
+        for i in range(3):
+            nc.vector.quantize_mx(
+                out=codes[i][:].bitcast(FP8X4), scales=planes[i][:], in_=grouped[i][:].rearrange("p c t -> p (c t)")
+            )
+            nc.tensor.matmul_mx(
+                out=sums[i][:],
+                lhsT=w_codes[:].bitcast(FP8X4),
+                lhsT_scale=w_planes[:],
+                rhs=codes[i][:].bitcast(FP8X4),
+                rhs_scale=planes[i][:],
+                start=True,
+                stop=True,
+            )
+            nc.scalar.activation(y[:, cols(i)], sums[i][:], SILU, bias=bias[:])
+
+        terms = [keep.tile([N, V], F32, name=f"term{d}", align_bytes=64) for d in range(D - 1)]
+        last = [keep.tile([N, HALF], F32, name=f"last{h}", align_bytes=64) for h in range(2)]
+        first_two = keep.tile([N, V], F32, name="first_two", align_bytes=64)
+        first_three = keep.tile([N, V], F32, name="first_three", align_bytes=64)
+        result = [keep.tile([N, HALF], F32, name=f"result{h}", align_bytes=64) for h in range(2)]
+
+        def half(h):
+            return slice(h * HALF, (h + 1) * HALF)
+
+        def last_term(h):
+            lines = slice(h * HALF // LINE, (h + 1) * HALF // LINE)
+            nc.vector.tensor_tensor(last[h][:], y[:].indirect(places[D - 1][:, lines]), gates[:, D - 1, half(h)], MULT)
+
+        for d in range(D - 1):
+            nc.vector.tensor_tensor(terms[d][:], y[:].indirect(places[d][:]), gates[:, d, :], MULT)
+        nc.vector.tensor_tensor(first_two[:], terms[0][:], terms[1][:], ADD)
+        last_term(0)
+        nc.vector.tensor_tensor(first_three[:], first_two[:], terms[2][:], ADD)
+        last_term(1)
+        for h in range(2):
+            nc.vector.tensor_tensor(result[h][:], first_three[:, half(h)], last[h][:], ADD)
+            (nc.scalar, nc.sync)[h].dma_start(out[:, half(h)], result[h][:])

@@ -5,7 +5,7 @@ import concourse.mybir as mybir
 K, T, D, S, V, N = 512, 1024, 4, 512, 256, 128
 P = 128
 PACK = 4
-PIECES = ((0, 256), (256, 384), (384, 512))
+PIECES = ((0, 128), (128, 256), (256, 384), (384, 512))
 LINE = 16
 HALF = V // 2
 
@@ -40,16 +40,15 @@ def tile_picked_sub_lin_silu_sub_e_kernel(tc, xT, w_words, w_scales, b, gate, of
         warm_out = keep.tile([P, 1], F32, name="warm_out")
 
         nc.vector.memset(warm[:], 0.0)
-        nc.gpsimd.memset(w_planes[:].bitcast(I32), 0)
         x_view = xT.rearrange("(p t) c -> p t c", t=PACK)
         nc.scalar.dma_start(x_rows[0][:], x_view[:, 0, :])
         nc.sync.dma_start(offsets[:], offs)
         for t in range(1, PACK):
             nc.sync.dma_start(x_rows[t][:], x_view[:, t, :])
         nc.scalar.activation(warm_out[:], warm[:], SILU)
-        for q in range(4):
-            (nc.gpsimd if q % 2 else nc.scalar).dma_start(w_planes[32 * q : 32 * q + 4, :].bitcast(I32), w_scales[0, 4 * q : 4 * q + 4, :].bitcast(I32))
         nc.sync.dma_start(w_codes[:].bitcast(I32), w_words[0].rearrange("p m r -> p (m r)").bitcast(I32))
+        for q in range(4):
+            (nc.gpsimd if q % 2 else nc.sync).dma_start(w_planes[32 * q : 32 * q + 4, :].bitcast(I32), w_scales[0, 4 * q : 4 * q + 4, :].bitcast(I32))
         nc.sync.dma_start(bias[:], b)
         nc.sync.dma_start(gates[:], gate.rearrange("d m v -> m d v"))
         for d, pos in enumerate((pos1, pos2, pos3, pos4)):
@@ -70,19 +69,28 @@ def tile_picked_sub_lin_silu_sub_e_kernel(tc, xT, w_words, w_scales, b, gate, of
             source = picked[:, t : t + 2, cols(i)].rearrange("p t c -> p c t")
             return grouped[i][:, :, t : t + 2], source
 
-        for t in range(PACK - 1):
-            nc.vector.tensor_copy(picked[:, t, :], x_rows[t][:].indirect(offsets[:]))
-            if t == 1:
-                for i in range(3):
-                    nc.scalar.copy(*pair(i, 0))
-        for i, (start, end) in enumerate(PIECES):
-            lines = slice(start // LINE, end // LINE)
-            nc.vector.tensor_copy(picked[:, PACK - 1, cols(i)], x_rows[PACK - 1][:].indirect(offsets[:, lines]))
-        nc.scalar.copy(*pair(0, 2))
-        nc.scalar.copy(*pair(2, 2))
-        nc.vector.tensor_copy(*pair(1, 2))
+        def gather(t, start, end):
+            nc.vector.tensor_copy(picked[:, t, start:end], x_rows[t][:].indirect(offsets[:, start // LINE : end // LINE]))
 
-        for i in range(3):
+        def gather_in_place(t, i):
+            start, end = PIECES[i]
+            nc.vector.tensor_copy(grouped[i][:, :, t], x_rows[t][:].indirect(offsets[:, start // LINE : end // LINE]))
+
+        gather(0, 0, S)
+        for first in (0, 2):
+            gather(1, PIECES[first][0], PIECES[first + 1][1])
+            for i in (first, first + 1):
+                nc.scalar.copy(*pair(i, 0))
+        gather(2, 0, S // 2)
+        for i in (2, 3):
+            gather_in_place(2, i)
+        for i in (0, 1):
+            gather(3, *PIECES[i])
+            nc.scalar.copy(*pair(i, 2))
+        for i in (2, 3):
+            gather_in_place(3, i)
+
+        for i in (2, 0, 3, 1):
             nc.vector.quantize_mx(
                 out=codes[i][:].bitcast(FP8X4), scales=planes[i][:], in_=grouped[i][:].rearrange("p c t -> p (c t)")
             )

@@ -5,8 +5,10 @@ import concourse.mybir as mybir
 K, T, D, S, V, N = 512, 1024, 4, 512, 256, 128
 P = 128
 PACK = 4
-PIECES = ((0, 128), (128, 256), (256, 384), (384, 512))
 LINE = 16
+QUADRANT = 32
+PIECE = 128
+SPLIT = S // 2
 HALF = V // 2
 
 FLOPS = 2 * K * S * N
@@ -31,9 +33,9 @@ def tile_picked_sub_lin_silu_sub_e_kernel(tc, xT, w_words, w_scales, b, gate, of
 
         offsets = keep.tile([P, S // LINE], U16, name="offsets")
         places = [keep.tile([P, V // LINE], U16, name=f"places{d}") for d in range(D)]
-        x_rows = [keep.tile([P, T], F32, name=f"x_rows{t}", align_bytes=64) for t in range(PACK)]
+        x_planes = [keep.tile([P, T], F32, name=f"x_plane{t}", align_bytes=64) for t in range(PACK)]
         w_codes = keep.tile([P, N], U32, name="w_codes", align_bytes=64)
-        w_planes = keep.tile([P, N], U8, name="w_planes", align_bytes=64)
+        w_scale = keep.tile([P, N], U8, name="w_scale", align_bytes=64)
         bias = keep.tile([P, 1], F32, name="bias")
         gates = keep.tile([P, D, V], F32, name="gates", align_bytes=64)
         warm = keep.tile([P, 1], F32, name="warm")
@@ -41,69 +43,68 @@ def tile_picked_sub_lin_silu_sub_e_kernel(tc, xT, w_words, w_scales, b, gate, of
 
         nc.vector.memset(warm[:], 0.0)
         x_view = xT.rearrange("(p t) c -> p t c", t=PACK)
-        nc.scalar.dma_start(x_rows[0][:], x_view[:, 0, :])
+        nc.scalar.dma_start(x_planes[0][:], x_view[:, 0, :])
         nc.sync.dma_start(offsets[:], offs)
         for t in range(1, PACK):
-            nc.sync.dma_start(x_rows[t][:], x_view[:, t, :])
+            nc.sync.dma_start(x_planes[t][:], x_view[:, t, :])
         nc.scalar.activation(warm_out[:], warm[:], SILU)
         nc.sync.dma_start(w_codes[:].bitcast(I32), w_words[0].rearrange("p m r -> p (m r)").bitcast(I32))
-        for q in range(4):
-            (nc.gpsimd if q % 2 else nc.sync).dma_start(w_planes[32 * q : 32 * q + 4, :].bitcast(I32), w_scales[0, 4 * q : 4 * q + 4, :].bitcast(I32))
+        for q in range(P // QUADRANT):
+            rows = w_scale[QUADRANT * q : QUADRANT * q + 4, :]
+            (nc.gpsimd if q % 2 else nc.sync).dma_start(rows.bitcast(I32), w_scales[0, 4 * q : 4 * q + 4, :].bitcast(I32))
         nc.sync.dma_start(bias[:], b)
         nc.sync.dma_start(gates[:], gate.rearrange("d m v -> m d v"))
         for d, pos in enumerate((pos1, pos2, pos3, pos4)):
             nc.sync.dma_start(places[d][:], pos)
 
+        pieces = S // PIECE
         picked = keep.tile([P, PACK, S], F32, name="picked", align_bytes=64)
-        widths = [end - start for start, end in PIECES]
-        grouped = [keep.tile([P, n, PACK], BF16, name=f"grouped{i}", align_bytes=64) for i, n in enumerate(widths)]
-        codes = [keep.tile([P, n], U32, name=f"codes{i}", align_bytes=64) for i, n in enumerate(widths)]
-        planes = [keep.tile([P, n], U8, name=f"planes{i}", align_bytes=64) for i, n in enumerate(widths)]
-        sums = [psum.tile([N, n], F32, name=f"sums{i}") for i, n in enumerate(widths)]
+        grouped = keep.tile([P, S, PACK], BF16, name="grouped", align_bytes=64)
+        codes = [keep.tile([P, PIECE], U32, name=f"codes{i}", align_bytes=64) for i in range(pieces)]
+        scales = [keep.tile([P, PIECE], U8, name=f"scales{i}", align_bytes=64) for i in range(pieces)]
+        sums = [psum.tile([N, PIECE], F32, name=f"sums{i}") for i in range(pieces)]
         y = keep.tile([N, S], F32, name="y", align_bytes=64)
 
-        def cols(i):
-            return slice(*PIECES[i])
-
-        def pair(i, t):
-            source = picked[:, t : t + 2, cols(i)].rearrange("p t c -> p c t")
-            return grouped[i][:, :, t : t + 2], source
+        def looked_up(t, start, end):
+            return x_planes[t][:].indirect(offsets[:, start // LINE : end // LINE])
 
         def gather(t, start, end):
-            nc.vector.tensor_copy(picked[:, t, start:end], x_rows[t][:].indirect(offsets[:, start // LINE : end // LINE]))
+            nc.vector.tensor_copy(picked[:, t, start:end], looked_up(t, start, end))
 
-        def gather_in_place(t, i):
-            start, end = PIECES[i]
-            nc.vector.tensor_copy(grouped[i][:, :, t], x_rows[t][:].indirect(offsets[:, start // LINE : end // LINE]))
+        def gather_in_place(t, start, end):
+            nc.vector.tensor_copy(grouped[:, start:end, t], looked_up(t, start, end))
+
+        def interleave(t, start, end):
+            nc.scalar.copy(grouped[:, start:end, t : t + 2], picked[:, t : t + 2, start:end].rearrange("p t c -> p c t"))
 
         gather(0, 0, S)
-        for first in (0, 2):
-            gather(1, PIECES[first][0], PIECES[first + 1][1])
-            for i in (first, first + 1):
-                nc.scalar.copy(*pair(i, 0))
-        gather(2, 0, S // 2)
-        for i in (2, 3):
-            gather_in_place(2, i)
-        for i in (0, 1):
-            gather(3, *PIECES[i])
-            nc.scalar.copy(*pair(i, 2))
-        for i in (2, 3):
-            gather_in_place(3, i)
+        for start in (0, S // 2):
+            gather(1, start, start + S // 2)
+            interleave(0, start, start + S // 2)
+        gather(2, 0, SPLIT)
+        gather_in_place(2, SPLIT, S)
+        for start in range(0, SPLIT, PIECE):
+            gather(3, start, start + PIECE)
+            interleave(2, start, start + PIECE)
+        for start in range(SPLIT, S, PIECE):
+            gather_in_place(3, start, start + PIECE)
 
-        for i in (2, 0, 3, 1):
+        for start in (*range(SPLIT, S, PIECE), *range(0, SPLIT, PIECE)):
+            i = start // PIECE
+            cols = slice(start, start + PIECE)
             nc.vector.quantize_mx(
-                out=codes[i][:].bitcast(FP8X4), scales=planes[i][:], in_=grouped[i][:].rearrange("p c t -> p (c t)")
+                out=codes[i][:].bitcast(FP8X4), scales=scales[i][:], in_=grouped[:, cols, :].rearrange("p c t -> p (c t)")
             )
             nc.tensor.matmul_mx(
                 out=sums[i][:],
                 lhsT=w_codes[:].bitcast(FP8X4),
-                lhsT_scale=w_planes[:],
+                lhsT_scale=w_scale[:],
                 rhs=codes[i][:].bitcast(FP8X4),
-                rhs_scale=planes[i][:],
+                rhs_scale=scales[i][:],
                 start=True,
                 stop=True,
             )
-            nc.scalar.activation(y[:, cols(i)], sums[i][:], SILU, bias=bias[:])
+            nc.scalar.activation(y[:, cols], sums[i][:], SILU, bias=bias[:])
 
         terms = [keep.tile([N, V], F32, name=f"term{d}", align_bytes=64) for d in range(D - 1)]
         last = [keep.tile([N, HALF], F32, name=f"last{h}", align_bytes=64) for h in range(2)]

@@ -1,6 +1,7 @@
 from contextlib import ExitStack
 
 import concourse.mybir as mybir
+from concourse.masks import make_identity
 
 K, T, D, S, V, N = 512, 1024, 4, 512, 256, 128
 P = 128
@@ -38,10 +39,13 @@ def tile_picked_sub_lin_silu_sub_e_kernel(tc, xT, w_words, w_scales, b, gate, of
         w_scale = keep.tile([P, N], U8, name="w_scale", align_bytes=64)
         bias = keep.tile([P, 1], F32, name="bias")
         gates = keep.tile([P, D, V], F32, name="gates", align_bytes=64)
+        identity = keep.tile([P, P], F32, name="identity", align_bytes=64)
         warm = keep.tile([P, 1], F32, name="warm")
         warm_out = keep.tile([P, 1], F32, name="warm_out")
 
         nc.vector.memset(warm[:], 0.0)
+        nc.vector.memset(identity[:], 0.0)
+        make_identity(nc, identity[:], nomemset=True)
         x_view = xT.rearrange("(p t) c -> p t c", t=PACK)
         nc.scalar.dma_start(x_planes[0][:], x_view[:, 0, :])
         nc.sync.dma_start(offsets[:], offs)
@@ -106,25 +110,33 @@ def tile_picked_sub_lin_silu_sub_e_kernel(tc, xT, w_words, w_scales, b, gate, of
             )
             nc.scalar.activation(y[:, cols], sums[i][:], SILU, bias=bias[:])
 
-        terms = [keep.tile([N, V], F32, name=f"term{d}", align_bytes=64) for d in range(D - 1)]
-        last = [keep.tile([N, HALF], F32, name=f"last{h}", align_bytes=64) for h in range(2)]
-        first_two = keep.tile([N, V], F32, name="first_two", align_bytes=64)
-        first_three = keep.tile([N, V], F32, name="first_three", align_bytes=64)
+        terms = [[keep.tile([N, HALF], F32, name=f"term{d}_{h}", align_bytes=64) for h in range(2)] for d in range(D)]
+        turned = psum.tile([HALF, N], F32, name="turned")
+        turned_sum = keep.tile([HALF, N], F32, name="turned_sum", align_bytes=64)
+        turned_back = psum.tile([N, HALF], F32, name="turned_back")
+        first_two = keep.tile([N, HALF], F32, name="first_two", align_bytes=64)
+        first_three = keep.tile([N, HALF], F32, name="first_three", align_bytes=64)
         result = [keep.tile([N, HALF], F32, name=f"result{h}", align_bytes=64) for h in range(2)]
 
         def half(h):
             return slice(h * HALF, (h + 1) * HALF)
 
-        def last_term(h):
-            lines = slice(h * HALF // LINE, (h + 1) * HALF // LINE)
-            nc.vector.tensor_tensor(last[h][:], y[:].indirect(places[D - 1][:, lines]), gates[:, D - 1, half(h)], MULT)
+        def term(d, h):
+            neighbours = y[:].indirect(places[d][:, h * HALF // LINE : (h + 1) * HALF // LINE])
+            nc.vector.tensor_tensor(terms[d][h][:], neighbours, gates[:, d, half(h)], MULT)
 
         for d in range(D - 1):
-            nc.vector.tensor_tensor(terms[d][:], y[:].indirect(places[d][:]), gates[:, d, :], MULT)
-        nc.vector.tensor_tensor(first_two[:], terms[0][:], terms[1][:], ADD)
-        last_term(0)
-        nc.vector.tensor_tensor(first_three[:], first_two[:], terms[2][:], ADD)
-        last_term(1)
-        for h in range(2):
-            nc.vector.tensor_tensor(result[h][:], first_three[:, half(h)], last[h][:], ADD)
-            (nc.scalar, nc.sync)[h].dma_start(out[:, half(h)], result[h][:])
+            term(d, 0)
+            nc.tensor.matmul(turned[:], terms[d][0][:], identity[:], is_transpose=True, start=d == 0, stop=d == D - 2)
+        nc.scalar.copy(turned_sum[:], turned[:])
+        nc.tensor.transpose(turned_back[:], turned_sum[:], identity[:])
+        for d in range(D - 1):
+            term(d, 1)
+        nc.vector.tensor_tensor(first_two[:], terms[0][1][:], terms[1][1][:], ADD)
+        term(D - 1, 1)
+        nc.vector.tensor_tensor(first_three[:], first_two[:], terms[2][1][:], ADD)
+        term(D - 1, 0)
+        nc.vector.tensor_tensor(result[1][:], first_three[:], terms[D - 1][1][:], ADD)
+        nc.scalar.dma_start(out[:, half(1)], result[1][:])
+        nc.vector.tensor_tensor(result[0][:], turned_back[:], terms[D - 1][0][:], ADD)
+        nc.sync.dma_start(out[:, half(0)], result[0][:])

@@ -110,7 +110,7 @@ def tile_picked_sub_lin_silu_sub_e_kernel(tc, xT, w_words, w_scales, b, gate, of
             )
             nc.scalar.activation(y[:, cols], sums[i][:], SILU, bias=bias[:])
 
-        terms = [[keep.tile([N, HALF], F32, name=f"term{d}_{h}", align_bytes=64) for h in range(2)] for d in range(D)]
+        terms = [keep.tile([N, V], F32, name=f"term{d}", align_bytes=64) for d in range(D)]
         turned = psum.tile([HALF, N], F32, name="turned")
         turned_sum = keep.tile([HALF, N], F32, name="turned_sum", align_bytes=64)
         turned_back = psum.tile([N, HALF], F32, name="turned_back")
@@ -121,22 +121,25 @@ def tile_picked_sub_lin_silu_sub_e_kernel(tc, xT, w_words, w_scales, b, gate, of
         def half(h):
             return slice(h * HALF, (h + 1) * HALF)
 
-        def term(d, h):
-            neighbours = y[:].indirect(places[d][:, h * HALF // LINE : (h + 1) * HALF // LINE])
-            nc.vector.tensor_tensor(terms[d][h][:], neighbours, gates[:, d, half(h)], MULT)
+        def term(d, cols):
+            neighbours = y[:].indirect(places[d][:, cols.start // LINE : cols.stop // LINE])
+            nc.vector.tensor_tensor(terms[d][:, cols], neighbours, gates[:, d, cols], MULT)
 
         for d in range(D - 1):
-            term(d, 0)
-            nc.tensor.matmul(turned[:], terms[d][0][:], identity[:], is_transpose=True, start=d == 0, stop=d == D - 2)
+            term(d, half(0))
+            nc.tensor.matmul(turned[:], terms[d][:, half(0)], identity[:], is_transpose=True, start=d == 0, stop=d == D - 2)
         nc.scalar.copy(turned_sum[:], turned[:])
         nc.tensor.transpose(turned_back[:], turned_sum[:], identity[:])
         for d in range(D - 1):
-            term(d, 1)
-        nc.vector.tensor_tensor(first_two[:], terms[0][1][:], terms[1][1][:], ADD)
-        term(D - 1, 1)
-        nc.vector.tensor_tensor(first_three[:], first_two[:], terms[2][1][:], ADD)
-        term(D - 1, 0)
-        nc.vector.tensor_tensor(result[1][:], first_three[:], terms[D - 1][1][:], ADD)
-        nc.scalar.dma_start(out[:, half(1)], result[1][:])
-        nc.vector.tensor_tensor(result[0][:], turned_back[:], terms[D - 1][0][:], ADD)
-        nc.sync.dma_start(out[:, half(0)], result[0][:])
+            term(d, half(1))
+        nc.vector.tensor_tensor(first_two[:], terms[0][:, half(1)], terms[1][:, half(1)], ADD)
+        term(D - 1, half(0))
+        nc.vector.tensor_tensor(first_three[:], first_two[:], terms[2][:, half(1)], ADD)
+        quarters = (slice(0, HALF // 2), slice(HALF // 2, HALF))
+        for cols in quarters:
+            term(D - 1, slice(HALF + cols.start, HALF + cols.stop))
+        nc.vector.tensor_tensor(result[0][:], turned_back[:], terms[D - 1][:, half(0)], ADD)
+        nc.scalar.dma_start(out[:, half(0)], result[0][:])
+        for cols in quarters:
+            nc.vector.tensor_tensor(result[1][:, cols], first_three[:, cols], terms[D - 1][:, HALF + cols.start : HALF + cols.stop], ADD)
+        nc.sync.dma_start(out[:, half(1)], result[1][:])

@@ -9,7 +9,6 @@ PACK = 4
 LINE = 16
 QUADRANT = 32
 PIECE = 128
-SPLIT = S // 2
 HALF = V // 2
 
 FLOPS = 2 * K * S * N
@@ -62,48 +61,47 @@ def tile_picked_sub_lin_silu_sub_e_kernel(tc, xT, w_words, w_scales, b, gate, of
             nc.sync.dma_start(places[d][:], pos)
 
         pieces = S // PIECE
-        picked = keep.tile([P, PACK, S], F32, name="picked", align_bytes=64)
-        grouped = keep.tile([P, S, PACK], BF16, name="grouped", align_bytes=64)
-        codes = [keep.tile([P, PIECE], U32, name=f"codes{i}", align_bytes=64) for i in range(pieces)]
+        last = pieces - 1
+        pairs = keep.tile([P, pieces, 2, PIECE], U32, name="pairs", align_bytes=64)
+        pair_halves = pairs[:].bitcast(BF16).rearrange("p i u (c e) -> p i u c e", e=2)
+        grouped = [keep.tile([P, PIECE, PACK], BF16, name=f"grouped{i}", tag=f"grouped{i}", align_bytes=64) for i in range(pieces)]
         scales = [keep.tile([P, PIECE], U8, name=f"scales{i}", align_bytes=64) for i in range(pieces)]
         sums = [psum.tile([N, PIECE], F32, name=f"sums{i}") for i in range(pieces)]
         y = keep.tile([N, S], F32, name="y", align_bytes=64)
 
-        def looked_up(t, start, end):
-            return x_planes[t][:].indirect(offsets[:, start // LINE : end // LINE])
+        def looked_up(t, first, end):
+            return x_planes[t][:].indirect(offsets[:, first * PIECE // LINE : end * PIECE // LINE])
 
-        def gather(t, start, end):
-            nc.vector.tensor_copy(picked[:, t, start:end], looked_up(t, start, end))
+        def gather_to_pairs(t, first, end):
+            nc.vector.tensor_copy(pair_halves[:, first:end, t // 2, :, t % 2], looked_up(t, first, end))
 
-        def gather_in_place(t, start, end):
-            nc.vector.tensor_copy(grouped[:, start:end, t], looked_up(t, start, end))
+        def gather_in_place(t):
+            nc.vector.tensor_copy(grouped[last][:, :, t], looked_up(t, last, pieces))
 
-        def interleave(t, start, end):
-            nc.scalar.copy(grouped[:, start:end, t : t + 2], picked[:, t : t + 2, start:end].rearrange("p t c -> p c t"))
+        def words(i):
+            return grouped[i][:].bitcast(U32)
 
-        gather(0, 0, S)
-        for start in (0, S // 2):
-            gather(1, start, start + S // 2)
-            interleave(0, start, start + S // 2)
-        gather(2, 0, SPLIT)
-        gather_in_place(2, SPLIT, S)
-        for start in range(0, SPLIT, PIECE):
-            gather(3, start, start + PIECE)
-            interleave(2, start, start + PIECE)
-        for start in range(SPLIT, S, PIECE):
-            gather_in_place(3, start, start + PIECE)
+        gather_to_pairs(0, 0, pieces)
+        gather_to_pairs(1, 0, pieces)
+        nc.scalar.copy(words(last)[:, :, 0], pairs[:, last, 0, :])
+        gather_to_pairs(2, 0, last)
+        gather_in_place(2)
+        for i in range(last):
+            gather_to_pairs(3, i, i + 1)
+            nc.scalar.copy(words(i), pairs[:, i, :, :].rearrange("p u c -> p c u"))
+        gather_in_place(3)
 
-        for start in (*range(SPLIT, S, PIECE), *range(0, SPLIT, PIECE)):
-            i = start // PIECE
-            cols = slice(start, start + PIECE)
+        for i in (0, last, 1, 2):
+            cols = slice(i * PIECE, (i + 1) * PIECE)
+            codes = keep.tile([P, PIECE], U32, name=f"codes{i}", tag="grouped0" if i == last else f"codes{i}", align_bytes=64)
             nc.vector.quantize_mx(
-                out=codes[i][:].bitcast(FP8X4), scales=scales[i][:], in_=grouped[:, cols, :].rearrange("p c t -> p (c t)")
+                out=codes[:].bitcast(FP8X4), scales=scales[i][:], in_=grouped[i][:].rearrange("p c t -> p (c t)")
             )
             nc.tensor.matmul_mx(
                 out=sums[i][:],
                 lhsT=w_codes[:].bitcast(FP8X4),
                 lhsT_scale=w_scale[:],
-                rhs=codes[i][:].bitcast(FP8X4),
+                rhs=codes[:].bitcast(FP8X4),
                 rhs_scale=scales[i][:],
                 start=True,
                 stop=True,

@@ -20,6 +20,7 @@ U32 = mybir.dt.uint32
 U16 = mybir.dt.uint16
 U8 = mybir.dt.uint8
 FP8X4 = mybir.dt.float8_e4m3fn_x4
+COPY = mybir.ActivationFunctionType.Copy
 SILU = mybir.ActivationFunctionType.Silu
 MULT = mybir.AluOpType.mult
 ADD = mybir.AluOpType.add
@@ -62,7 +63,7 @@ def tile_picked_sub_lin_silu_sub_e_kernel(tc, xT, w_words, w_scales, b, gate, of
 
         pieces = S // PIECE
         last = pieces - 1
-        pairs = keep.tile([P, pieces, 2, PIECE], U32, name="pairs", align_bytes=64)
+        pairs = keep.tile([P, last, 2, PIECE], U32, name="pairs", align_bytes=64)
         pair_halves = pairs[:].bitcast(BF16).rearrange("p i u (c e) -> p i u c e", e=2)
         grouped = [keep.tile([P, PIECE, PACK], BF16, name=f"grouped{i}", tag=f"grouped{i}", align_bytes=64) for i in range(pieces)]
         scales = [keep.tile([P, PIECE], U8, name=f"scales{i}", align_bytes=64) for i in range(pieces)]
@@ -81,9 +82,11 @@ def tile_picked_sub_lin_silu_sub_e_kernel(tc, xT, w_words, w_scales, b, gate, of
         def words(i):
             return grouped[i][:].bitcast(U32)
 
-        gather_to_pairs(0, 0, pieces)
-        gather_to_pairs(1, 0, pieces)
-        nc.scalar.copy(words(last)[:, :, 0], pairs[:, last, 0, :])
+        for t in range(2):
+            gather_to_pairs(t, 0, last)
+            rounded = keep.tile([P, T], BF16, name=f"rounded{t}", align_bytes=64)
+            nc.scalar.copy(rounded[:], x_planes[t][:])
+            nc.scalar.activation(grouped[last][:, :, t], rounded[:].indirect(offsets[:, last * PIECE // LINE :]), COPY)
         gather_to_pairs(2, 0, last)
         gather_in_place(2)
         for i in range(last):

@@ -9,6 +9,7 @@ PACK = 4
 LINE = 16
 QUADRANT = 32
 PIECE = 128
+LOAD_ORDER = (0, 2, 1, 3)
 HALF = V // 2
 
 FLOPS = 2 * K * S * N
@@ -49,7 +50,7 @@ def tile_picked_sub_lin_silu_sub_e_kernel(tc, xT, w_words, w_scales, b, gate, of
         x_view = xT.rearrange("(p t) c -> p t c", t=PACK)
         nc.scalar.dma_start(x_planes[0][:], x_view[:, 0, :])
         nc.sync.dma_start(offsets[:], offs)
-        for t in range(1, PACK):
+        for t in LOAD_ORDER[1:]:
             nc.sync.dma_start(x_planes[t][:], x_view[:, t, :])
         nc.scalar.activation(warm_out[:], warm[:], SILU)
         nc.sync.dma_start(w_codes[:].bitcast(I32), w_words[0].rearrange("p m r -> p (m r)").bitcast(I32))
@@ -82,13 +83,14 @@ def tile_picked_sub_lin_silu_sub_e_kernel(tc, xT, w_words, w_scales, b, gate, of
         def words(i):
             return grouped[i][:].bitcast(U32)
 
-        for t in range(2):
+        for t in LOAD_ORDER[:-1]:
             gather_to_pairs(t, 0, last)
-            rounded = keep.tile([P, T], BF16, name=f"rounded{t}", align_bytes=64)
-            nc.scalar.copy(rounded[:], x_planes[t][:])
-            nc.scalar.activation(grouped[last][:, :, t], rounded[:].indirect(offsets[:, last * PIECE // LINE :]), COPY)
-        gather_to_pairs(2, 0, last)
-        gather_in_place(2)
+            if t == 2:
+                gather_in_place(t)
+            else:
+                rounded = keep.tile([P, T], BF16, name=f"rounded{t}", align_bytes=64)
+                nc.scalar.copy(rounded[:], x_planes[t][:])
+                nc.scalar.activation(grouped[last][:, :, t], rounded[:].indirect(offsets[:, last * PIECE // LINE :]), COPY)
         for i in range(last):
             gather_to_pairs(3, i, i + 1)
             nc.scalar.copy(words(i), pairs[:, i, :, :].rearrange("p u c -> p c u"))

@@ -64,8 +64,12 @@ def tile_picked_sub_lin_silu_sub_e_kernel(tc, xT, w_words, w_scales, b, gate, of
 
         pieces = S // PIECE
         last = pieces - 1
-        pairs = keep.tile([P, last, 2, PIECE], U32, name="pairs", align_bytes=64)
-        pair_halves = pairs[:].bitcast(BF16).rearrange("p i u (c e) -> p i u c e", e=2)
+        first_pairs = keep.tile([P, 1, 2, PIECE], U32, name="first_pairs", tag="first_pairs", align_bytes=64)
+        other_pairs = keep.tile([P, last - 1, 2, PIECE], U32, name="other_pairs", align_bytes=64)
+
+        def pairs(first, end):
+            return first_pairs[:] if first == 0 else other_pairs[:, first - 1 : end - 1, :, :]
+
         grouped = [keep.tile([P, PIECE, PACK], BF16, name=f"grouped{i}", tag=f"grouped{i}", align_bytes=64) for i in range(pieces)]
         scales = [keep.tile([P, PIECE], U8, name=f"scales{i}", align_bytes=64) for i in range(pieces)]
         sums = [psum.tile([N, PIECE], F32, name=f"sums{i}") for i in range(pieces)]
@@ -75,7 +79,7 @@ def tile_picked_sub_lin_silu_sub_e_kernel(tc, xT, w_words, w_scales, b, gate, of
             return x_planes[t][:].indirect(offsets[:, first * PIECE // LINE : end * PIECE // LINE])
 
         def gather_to_pairs(t, first, end):
-            nc.vector.tensor_copy(pair_halves[:, first:end, t // 2, :, t % 2], looked_up(t, first, end))
+            nc.vector.tensor_copy(pairs(first, end).bitcast(BF16).rearrange("p i u (c e) -> p i u c e", e=2)[:, :, t // 2, :, t % 2], looked_up(t, first, end))
 
         def gather_in_place(t):
             nc.vector.tensor_copy(grouped[last][:, :, t], looked_up(t, last, pieces))
@@ -84,7 +88,8 @@ def tile_picked_sub_lin_silu_sub_e_kernel(tc, xT, w_words, w_scales, b, gate, of
             return grouped[i][:].bitcast(U32)
 
         for t in LOAD_ORDER[:-1]:
-            gather_to_pairs(t, 0, last)
+            gather_to_pairs(t, 0, 1)
+            gather_to_pairs(t, 1, last)
             if t == 2:
                 gather_in_place(t)
             else:
@@ -93,12 +98,12 @@ def tile_picked_sub_lin_silu_sub_e_kernel(tc, xT, w_words, w_scales, b, gate, of
                 nc.scalar.activation(grouped[last][:, :, t], rounded[:].indirect(offsets[:, last * PIECE // LINE :]), COPY)
         for i in range(last):
             gather_to_pairs(3, i, i + 1)
-            nc.scalar.copy(words(i), pairs[:, i, :, :].rearrange("p u c -> p c u"))
+            nc.scalar.copy(words(i), pairs(i, i + 1).rearrange("p i u c -> p (i c) u"))
         gather_in_place(3)
 
         for i in (0, last, 1, 2):
             cols = slice(i * PIECE, (i + 1) * PIECE)
-            codes = keep.tile([P, PIECE], U32, name=f"codes{i}", tag="grouped0" if i == last else f"codes{i}", align_bytes=64)
+            codes = keep.tile([P, PIECE], U32, name=f"codes{i}", tag="first_pairs" if i == last else f"codes{i}", align_bytes=64)
             nc.vector.quantize_mx(
                 out=codes[:].bitcast(FP8X4), scales=scales[i][:], in_=grouped[i][:].rearrange("p c t -> p (c t)")
             )

@@ -118,36 +118,38 @@ def tile_picked_sub_lin_silu_sub_e_kernel(tc, xT, w_words, w_scales, b, gate, of
             )
             nc.scalar.activation(y[:, cols], sums[i][:], SILU, bias=bias[:])
 
-        terms = [keep.tile([N, V], F32, name=f"term{d}", align_bytes=64) for d in range(D)]
+        terms = [keep.tile([N, V], F32, name=f"term{d}", align_bytes=64) for d in range(D - 1)]
         turned = psum.tile([HALF, N], F32, name="turned")
         turned_sum = keep.tile([HALF, N], F32, name="turned_sum", align_bytes=64)
         turned_back = psum.tile([N, HALF], F32, name="turned_back")
         first_two = keep.tile([N, HALF], F32, name="first_two", align_bytes=64)
         first_three = keep.tile([N, HALF], F32, name="first_three", align_bytes=64)
-        result = [keep.tile([N, HALF], F32, name=f"result{h}", align_bytes=64) for h in range(2)]
+        result = keep.tile([N, HALF], F32, name="result", align_bytes=64)
 
         def half(h):
             return slice(h * HALF, (h + 1) * HALF)
 
-        def term(d, cols):
+        def term(d, cols, into):
             neighbours = y[:].indirect(places[d][:, cols.start // LINE : cols.stop // LINE])
-            nc.vector.tensor_tensor(terms[d][:, cols], neighbours, gates[:, d, cols], MULT)
+            nc.vector.tensor_tensor(into, neighbours, gates[:, d, cols], MULT)
 
         for d in range(D - 1):
-            term(d, half(0))
+            term(d, half(0), terms[d][:, half(0)])
             nc.tensor.matmul(turned[:], terms[d][:, half(0)], identity[:], is_transpose=True, start=d == 0, stop=d == D - 2)
         nc.scalar.copy(turned_sum[:], turned[:])
         nc.tensor.transpose(turned_back[:], turned_sum[:], identity[:])
         for d in range(D - 1):
-            term(d, half(1))
+            term(d, half(1), terms[d][:, half(1)])
         nc.vector.tensor_tensor(first_two[:], terms[0][:, half(1)], terms[1][:, half(1)], ADD)
-        term(D - 1, half(0))
+        last_term0 = gates[:, 1, half(1)]
+        last_term1 = terms[0][:, half(1)]
+        term(D - 1, half(0), last_term0)
         nc.vector.tensor_tensor(first_three[:], first_two[:], terms[2][:, half(1)], ADD)
         quarters = (slice(0, HALF // 2), slice(HALF // 2, HALF))
         for cols in quarters:
-            term(D - 1, slice(HALF + cols.start, HALF + cols.stop))
-        nc.vector.tensor_tensor(result[0][:], turned_back[:], terms[D - 1][:, half(0)], ADD)
-        nc.scalar.dma_start(out[:, half(0)], result[0][:])
+            term(D - 1, slice(HALF + cols.start, HALF + cols.stop), last_term1[:, cols])
+        nc.vector.tensor_tensor(result[:], turned_back[:], last_term0, ADD)
+        nc.scalar.dma_start(out[:, half(0)], result[:])
         for cols in quarters:
-            nc.vector.tensor_tensor(result[1][:, cols], first_three[:, cols], terms[D - 1][:, HALF + cols.start : HALF + cols.stop], ADD)
-        nc.sync.dma_start(out[:, half(1)], result[1][:])
+            nc.vector.tensor_tensor(turned_sum[:, cols], first_three[:, cols], last_term1[:, cols], ADD)
+        nc.sync.dma_start(out[:, half(1)], turned_sum[:])

@@ -64,11 +64,11 @@ def tile_picked_sub_lin_silu_sub_e_kernel(tc, xT, w_words, w_scales, b, gate, of
 
         pieces = S // PIECE
         last = pieces - 1
-        first_pairs = keep.tile([P, 1, 2, PIECE], U32, name="first_pairs", tag="first_pairs", align_bytes=64)
-        other_pairs = keep.tile([P, last - 1, 2, PIECE], U32, name="other_pairs", align_bytes=64)
+        first_pairs = keep.tile([P, 2, 2, PIECE], U32, name="first_pairs", tag="first_pairs", align_bytes=64)
+        other_pairs = keep.tile([P, 1, 2, PIECE], U32, name="other_pairs", align_bytes=64)
 
         def pairs(first, end):
-            return first_pairs[:] if first == 0 else other_pairs[:, first - 1 : end - 1, :, :]
+            return first_pairs[:, first:end, :, :] if first < 2 else other_pairs[:]
 
         grouped = [keep.tile([P, PIECE, PACK], BF16, name=f"grouped{i}", tag=f"grouped{i}", align_bytes=64) for i in range(pieces)]
         scales = [keep.tile([P, PIECE], U8, name=f"scales{i}", align_bytes=64) for i in range(pieces)]
@@ -88,8 +88,8 @@ def tile_picked_sub_lin_silu_sub_e_kernel(tc, xT, w_words, w_scales, b, gate, of
             return grouped[i][:].bitcast(U32)
 
         for t in LOAD_ORDER[:-1]:
-            gather_to_pairs(t, 0, 1)
-            gather_to_pairs(t, 1, last)
+            gather_to_pairs(t, 0, 2)
+            gather_to_pairs(t, 2, last)
             if t == 2:
                 gather_in_place(t)
             else:
@@ -101,7 +101,7 @@ def tile_picked_sub_lin_silu_sub_e_kernel(tc, xT, w_words, w_scales, b, gate, of
             nc.scalar.copy(words(i), pairs(i, i + 1).rearrange("p i u c -> p (i c) u"))
         gather_in_place(3)
 
-        for i in (0, last, 1, 2):
+        for i in (0, 1, last, 2):
             cols = slice(i * PIECE, (i + 1) * PIECE)
             codes = keep.tile([P, PIECE], U32, name=f"codes{i}", tag="first_pairs" if i == last else f"codes{i}", align_bytes=64)
             nc.vector.quantize_mx(
@@ -124,7 +124,6 @@ def tile_picked_sub_lin_silu_sub_e_kernel(tc, xT, w_words, w_scales, b, gate, of
         turned_back = psum.tile([N, HALF], F32, name="turned_back")
         first_two = keep.tile([N, HALF], F32, name="first_two", align_bytes=64)
         first_three = keep.tile([N, HALF], F32, name="first_three", align_bytes=64)
-        result = keep.tile([N, HALF], F32, name="result", align_bytes=64)
 
         def half(h):
             return slice(h * HALF, (h + 1) * HALF)
@@ -141,15 +140,16 @@ def tile_picked_sub_lin_silu_sub_e_kernel(tc, xT, w_words, w_scales, b, gate, of
         for d in range(D - 1):
             term(d, half(1), terms[d][:, half(1)])
         nc.vector.tensor_tensor(first_two[:], terms[0][:, half(1)], terms[1][:, half(1)], ADD)
-        last_term0 = gates[:, 1, half(1)]
-        last_term1 = terms[0][:, half(1)]
-        term(D - 1, half(0), last_term0)
-        nc.vector.tensor_tensor(first_three[:], first_two[:], terms[2][:, half(1)], ADD)
+        last_term1 = gates[:, 1, half(1)]
+        last_term0 = terms[0][:, half(1)]
         quarters = (slice(0, HALF // 2), slice(HALF // 2, HALF))
+        result = gates[:].rearrange("p d v -> p (d v)")[:, (D - 1) * V - HALF // 2 : (D - 1) * V + HALF // 2]
+        term(D - 1, half(1), last_term1)
+        nc.vector.tensor_tensor(first_three[:], first_two[:], terms[2][:, half(1)], ADD)
         for cols in quarters:
-            term(D - 1, slice(HALF + cols.start, HALF + cols.stop), last_term1[:, cols])
-        nc.vector.tensor_tensor(result[:], turned_back[:], last_term0, ADD)
-        nc.scalar.dma_start(out[:, half(0)], result[:])
+            term(D - 1, cols, last_term0[:, cols])
+        nc.vector.tensor_tensor(result, first_three[:], last_term1, ADD)
+        nc.scalar.dma_start(out[:, half(1)], result)
         for cols in quarters:
-            nc.vector.tensor_tensor(turned_sum[:, cols], first_three[:, cols], last_term1[:, cols], ADD)
-        nc.sync.dma_start(out[:, half(1)], turned_sum[:])
+            nc.vector.tensor_tensor(turned_sum[:, cols], turned_back[:, cols], last_term0[:, cols], ADD)
+        nc.sync.dma_start(out[:, half(0)], turned_sum[:])

@@ -35,11 +35,10 @@ def tile_picked_sub_lin_silu_sub_e_kernel(tc, xT, w_words, w_scales, b, gate, of
 
         offsets = keep.tile([P, S // LINE], U16, name="offsets")
         places = [keep.tile([P, V // LINE], U16, name=f"places{d}") for d in range(D)]
-        x_planes = [keep.tile([P, T], F32, name=f"x_plane{t}", align_bytes=64) for t in range(PACK)]
+        x_planes = [keep.tile([P, T], F32, name=f"x_plane{t}", tag=f"x_plane{t}", align_bytes=64) for t in range(PACK)]
         w_codes = keep.tile([P, N], U32, name="w_codes", align_bytes=64)
         w_scale = keep.tile([P, N], U8, name="w_scale", align_bytes=64)
-        bias = keep.tile([P, 1], F32, name="bias")
-        gates = keep.tile([P, D, V], F32, name="gates", align_bytes=64)
+        gates = [keep.tile([P, D, HALF], F32, name=f"gates{h}", align_bytes=64) for h in range(2)]
         identity = keep.tile([P, P], F32, name="identity", align_bytes=64)
         warm = keep.tile([P, 1], F32, name="warm")
         warm_out = keep.tile([P, 1], F32, name="warm_out")
@@ -57,10 +56,12 @@ def tile_picked_sub_lin_silu_sub_e_kernel(tc, xT, w_words, w_scales, b, gate, of
         for q in range(P // QUADRANT):
             rows = w_scale[QUADRANT * q : QUADRANT * q + 4, :]
             (nc.gpsimd if q % 2 else nc.sync).dma_start(rows.bitcast(I32), w_scales[0, 4 * q : 4 * q + 4, :].bitcast(I32))
-        nc.sync.dma_start(bias[:], b)
-        nc.sync.dma_start(gates[:], gate.rearrange("d m v -> m d v"))
-        for d, pos in enumerate((pos1, pos2, pos3, pos4)):
+        gate_rows = gate.rearrange("d m v -> m d v")
+        nc.sync.dma_start(gates[0][:], gate_rows[:, :, :HALF])
+        for d, pos in enumerate((pos1, pos2, pos3)):
             nc.sync.dma_start(places[d][:], pos)
+        nc.sync.dma_start(gates[1][:], gate_rows[:, :, HALF:])
+        nc.sync.dma_start(places[D - 1][:], pos4)
 
         pieces = S // PIECE
         last = pieces - 1
@@ -96,6 +97,8 @@ def tile_picked_sub_lin_silu_sub_e_kernel(tc, xT, w_words, w_scales, b, gate, of
                 rounded = keep.tile([P, T], BF16, name=f"rounded{t}", align_bytes=64)
                 nc.scalar.copy(rounded[:], x_planes[t][:])
                 nc.scalar.activation(grouped[last][:, :, t], rounded[:].indirect(offsets[:, last * PIECE // LINE :]), COPY)
+        bias = keep.tile([P, 1], F32, name="bias", tag="x_plane0", align_bytes=64)
+        nc.gpsimd.dma_start(bias[:], b)
         for i in range(last):
             gather_to_pairs(3, i, i + 1)
             nc.scalar.copy(words(i), pairs(i, i + 1).rearrange("p i u c -> p (i c) u"))
@@ -130,7 +133,7 @@ def tile_picked_sub_lin_silu_sub_e_kernel(tc, xT, w_words, w_scales, b, gate, of
 
         def term(d, cols, into):
             neighbours = y[:].indirect(places[d][:, cols.start // LINE : cols.stop // LINE])
-            nc.vector.tensor_tensor(into, neighbours, gates[:, d, cols], MULT)
+            nc.vector.tensor_tensor(into, neighbours, gates[cols.start // HALF][:, d, cols.start % HALF : cols.start % HALF + cols.stop - cols.start], MULT)
 
         for d in range(D - 1):
             term(d, half(0), terms[d][:, half(0)])
@@ -140,10 +143,10 @@ def tile_picked_sub_lin_silu_sub_e_kernel(tc, xT, w_words, w_scales, b, gate, of
         for d in range(D - 1):
             term(d, half(1), terms[d][:, half(1)])
         nc.vector.tensor_tensor(first_two[:], terms[0][:, half(1)], terms[1][:, half(1)], ADD)
-        last_term1 = gates[:, 1, half(1)]
+        last_term1 = gates[1][:, 1, :]
         last_term0 = terms[0][:, half(1)]
         quarters = (slice(0, HALF // 2), slice(HALF // 2, HALF))
-        result = gates[:].rearrange("p d v -> p (d v)")[:, (D - 1) * V - HALF // 2 : (D - 1) * V + HALF // 2]
+        result = gates[0][:].rearrange("p d v -> p (d v)")[:, (D - 1) * HALF - HALF // 2 : (D - 1) * HALF + HALF // 2]
         term(D - 1, half(1), last_term1)
         nc.vector.tensor_tensor(first_three[:], first_two[:], terms[2][:, half(1)], ADD)
         for cols in quarters:

@@ -9,7 +9,6 @@ PACK = 4
 LINE = 16
 QUADRANT = 32
 PIECE = 128
-LOAD_ORDER = (0, 2, 1, 3)
 HALF = V // 2
 
 FLOPS = 2 * K * S * N
@@ -33,15 +32,19 @@ def tile_picked_sub_lin_silu_sub_e_kernel(tc, xT, w_words, w_scales, b, gate, of
         keep = ctx.enter_context(tc.tile_pool(name="keep", bufs=1))
         psum = ctx.enter_context(tc.psum_pool(name="psum", bufs=1))
 
+        def sbuf(name, shape, dtype, tag=None):
+            return keep.tile(shape, dtype, name=name, tag=tag or name, align_bytes=64)
+
         offsets = keep.tile([P, S // LINE], U16, name="offsets")
         places = [keep.tile([P, V // LINE], U16, name=f"places{d}") for d in range(D)]
-        x_planes = [keep.tile([P, T], F32, name=f"x_plane{t}", tag=f"x_plane{t}", align_bytes=64) for t in range(PACK)]
-        w_codes = keep.tile([P, N], U32, name="w_codes", align_bytes=64)
-        w_scale = keep.tile([P, N], U8, name="w_scale", align_bytes=64)
-        gates = [keep.tile([P, D, HALF], F32, name=f"gates{h}", align_bytes=64) for h in range(2)]
-        identity = keep.tile([P, P], F32, name="identity", align_bytes=64)
-        warm = keep.tile([P, 1], F32, name="warm")
-        warm_out = keep.tile([P, 1], F32, name="warm_out")
+        x_planes = [sbuf(f"x_plane{t}", [P, T], F32) for t in range(PACK)]
+        w_codes = sbuf("w_codes", [P, N], U32)
+        w_scale = sbuf("w_scale", [P, N], U8)
+        gates_fused = sbuf("gates_fused", [P, 2, V], F32)
+        gates_after = sbuf("gates_after", [P, 2, HALF], F32)
+        identity = sbuf("identity", [P, P], F32)
+        warm = sbuf("warm", [P, 1], F32)
+        warm_out = sbuf("warm_out", [P, 1], F32)
 
         nc.vector.memset(warm[:], 0.0)
         nc.vector.memset(identity[:], 0.0)
@@ -49,7 +52,7 @@ def tile_picked_sub_lin_silu_sub_e_kernel(tc, xT, w_words, w_scales, b, gate, of
         x_view = xT.rearrange("(p t) c -> p t c", t=PACK)
         nc.scalar.dma_start(x_planes[0][:], x_view[:, 0, :])
         nc.sync.dma_start(offsets[:], offs)
-        for t in LOAD_ORDER[1:]:
+        for t in (2, 1, 3):
             nc.sync.dma_start(x_planes[t][:], x_view[:, t, :])
         nc.scalar.activation(warm_out[:], warm[:], SILU)
         nc.sync.dma_start(w_codes[:].bitcast(I32), w_words[0].rearrange("p m r -> p (m r)").bitcast(I32))
@@ -57,59 +60,60 @@ def tile_picked_sub_lin_silu_sub_e_kernel(tc, xT, w_words, w_scales, b, gate, of
             rows = w_scale[QUADRANT * q : QUADRANT * q + 4, :]
             (nc.gpsimd if q % 2 else nc.sync).dma_start(rows.bitcast(I32), w_scales[0, 4 * q : 4 * q + 4, :].bitcast(I32))
         gate_rows = gate.rearrange("d m v -> m d v")
-        nc.sync.dma_start(gates[0][:], gate_rows[:, :, :HALF])
-        for d, pos in enumerate((pos1, pos2, pos3)):
+        nc.sync.dma_start(gates_fused[:], gate_rows[:, 2:, :])
+        for d, pos in ((0, pos1), (2, pos3), (1, pos2), (3, pos4)):
             nc.sync.dma_start(places[d][:], pos)
-        nc.sync.dma_start(gates[1][:], gate_rows[:, :, HALF:])
-        nc.sync.dma_start(places[D - 1][:], pos4)
+        nc.sync.dma_start(gates_after[:], gate_rows[:, :2, HALF:])
 
         pieces = S // PIECE
         last = pieces - 1
-        first_pairs = keep.tile([P, 2, 2, PIECE], U32, name="first_pairs", tag="first_pairs", align_bytes=64)
-        other_pairs = keep.tile([P, 1, 2, PIECE], U32, name="other_pairs", align_bytes=64)
+        first_pairs = sbuf("first_pairs", [P, 2, 2, PIECE], U32)
+        other_pairs = sbuf("other_pairs", [P, 1, 2, PIECE], U32)
 
         def pairs(first, end):
             return first_pairs[:, first:end, :, :] if first < 2 else other_pairs[:]
 
-        grouped = [keep.tile([P, PIECE, PACK], BF16, name=f"grouped{i}", tag=f"grouped{i}", align_bytes=64) for i in range(pieces)]
-        scales = [keep.tile([P, PIECE], U8, name=f"scales{i}", align_bytes=64) for i in range(pieces)]
+        def pair_halves(first, end):
+            return pairs(first, end).bitcast(BF16).rearrange("p i u (c e) -> p i u c e", e=2)
+
+        grouped = [sbuf(f"grouped{i}", [P, PIECE, PACK], BF16) for i in range(pieces)]
+        scales = [sbuf(f"scales{i}", [P, PIECE], U8) for i in range(pieces)]
         sums = [psum.tile([N, PIECE], F32, name=f"sums{i}") for i in range(pieces)]
-        y = keep.tile([N, S], F32, name="y", align_bytes=64)
+        plain = sbuf("plain", [P, 2, 2 * PIECE], BF16)
+        y = sbuf("y", [N, S], F32)
 
         def looked_up(t, first, end):
             return x_planes[t][:].indirect(offsets[:, first * PIECE // LINE : end * PIECE // LINE])
 
         def gather_to_pairs(t, first, end):
-            nc.vector.tensor_copy(pairs(first, end).bitcast(BF16).rearrange("p i u (c e) -> p i u c e", e=2)[:, :, t // 2, :, t % 2], looked_up(t, first, end))
+            nc.vector.tensor_copy(pair_halves(first, end)[:, :, t // 2, :, t % 2], looked_up(t, first, end))
 
         def gather_in_place(t):
             nc.vector.tensor_copy(grouped[last][:, :, t], looked_up(t, last, pieces))
 
-        def words(i):
-            return grouped[i][:].bitcast(U32)
-
-        for t in LOAD_ORDER[:-1]:
-            gather_to_pairs(t, 0, 2)
-            gather_to_pairs(t, 2, last)
-            if t == 2:
-                gather_in_place(t)
-            else:
-                rounded = keep.tile([P, T], BF16, name=f"rounded{t}", align_bytes=64)
-                nc.scalar.copy(rounded[:], x_planes[t][:])
-                nc.scalar.activation(grouped[last][:, :, t], rounded[:].indirect(offsets[:, last * PIECE // LINE :]), COPY)
-        bias = keep.tile([P, 1], F32, name="bias", tag="x_plane0", align_bytes=64)
-        nc.gpsimd.dma_start(bias[:], b)
+        gather_to_pairs(0, 0, 2)
+        nc.scalar.activation(plain[:, 0, :], looked_up(0, 2, pieces), COPY)
+        gather_to_pairs(2, 0, 2)
+        gather_to_pairs(2, 2, last)
+        gather_in_place(2)
+        gather_to_pairs(1, 0, 2)
+        nc.scalar.activation(plain[:, 1, :], looked_up(1, 2, pieces), COPY)
+        nc.scalar.copy(pair_halves(2, last)[:, 0, 0, :, :], plain[:, :, :PIECE].rearrange("p e c -> p c e"))
+        nc.scalar.copy(grouped[last][:, :, :2], plain[:, :, PIECE:].rearrange("p e c -> p c e"))
+        columns = sbuf("columns", [P, 16], F32, tag="x_plane0")
+        bias = columns[:, 0:1]
+        gates_turned = columns[:, 8:10]
+        nc.gpsimd.dma_start(bias, b)
+        with nc.allow_non_contiguous_dma(reason="one value of gate to a partition"):
+            nc.gpsimd.dma_start(gates_turned, gate[:2, 0, :HALF].rearrange("d v -> v d"))
         for i in range(last):
             gather_to_pairs(3, i, i + 1)
-            nc.scalar.copy(words(i), pairs(i, i + 1).rearrange("p i u c -> p (i c) u"))
+            nc.scalar.copy(grouped[i][:].bitcast(U32), pairs(i, i + 1).rearrange("p i u c -> p (i c) u"))
         gather_in_place(3)
 
         for i in (0, 1, last, 2):
-            cols = slice(i * PIECE, (i + 1) * PIECE)
-            codes = keep.tile([P, PIECE], U32, name=f"codes{i}", tag="first_pairs" if i == last else f"codes{i}", align_bytes=64)
-            nc.vector.quantize_mx(
-                out=codes[:].bitcast(FP8X4), scales=scales[i][:], in_=grouped[i][:].rearrange("p c t -> p (c t)")
-            )
+            codes = sbuf(f"codes{i}", [P, PIECE], U32, tag="first_pairs" if i == last else None)
+            nc.vector.quantize_mx(out=codes[:].bitcast(FP8X4), scales=scales[i][:], in_=grouped[i][:].rearrange("p c t -> p (c t)"))
             nc.tensor.matmul_mx(
                 out=sums[i][:],
                 lhsT=w_codes[:].bitcast(FP8X4),
@@ -119,40 +123,40 @@ def tile_picked_sub_lin_silu_sub_e_kernel(tc, xT, w_words, w_scales, b, gate, of
                 start=True,
                 stop=True,
             )
-            nc.scalar.activation(y[:, cols], sums[i][:], SILU, bias=bias[:])
-
-        terms = [keep.tile([N, V], F32, name=f"term{d}", align_bytes=64) for d in range(D - 1)]
-        turned = psum.tile([HALF, N], F32, name="turned")
-        turned_sum = keep.tile([HALF, N], F32, name="turned_sum", align_bytes=64)
-        turned_back = psum.tile([N, HALF], F32, name="turned_back")
-        first_two = keep.tile([N, HALF], F32, name="first_two", align_bytes=64)
-        first_three = keep.tile([N, HALF], F32, name="first_three", align_bytes=64)
+            nc.scalar.activation(y[:, i * PIECE : (i + 1) * PIECE], sums[i][:], SILU, bias=bias)
 
         def half(h):
             return slice(h * HALF, (h + 1) * HALF)
 
-        def term(d, cols, into):
-            neighbours = y[:].indirect(places[d][:, cols.start // LINE : cols.stop // LINE])
-            nc.vector.tensor_tensor(into, neighbours, gates[cols.start // HALF][:, d, cols.start % HALF : cols.start % HALF + cols.stop - cols.start], MULT)
+        def neighbours(d, h):
+            return y[:].indirect(places[d][:, h * HALF // LINE : (h + 1) * HALF // LINE])
 
-        for d in range(D - 1):
-            term(d, half(0), terms[d][:, half(0)])
-            nc.tensor.matmul(turned[:], terms[d][:, half(0)], identity[:], is_transpose=True, start=d == 0, stop=d == D - 2)
-        nc.scalar.copy(turned_sum[:], turned[:])
-        nc.tensor.transpose(turned_back[:], turned_sum[:], identity[:])
-        for d in range(D - 1):
-            term(d, half(1), terms[d][:, half(1)])
-        nc.vector.tensor_tensor(first_two[:], terms[0][:, half(1)], terms[1][:, half(1)], ADD)
-        last_term1 = gates[1][:, 1, :]
-        last_term0 = terms[0][:, half(1)]
-        quarters = (slice(0, HALF // 2), slice(HALF // 2, HALF))
-        result = gates[0][:].rearrange("p d v -> p (d v)")[:, (D - 1) * HALF - HALF // 2 : (D - 1) * HALF + HALF // 2]
-        term(D - 1, half(1), last_term1)
-        nc.vector.tensor_tensor(first_three[:], first_two[:], terms[2][:, half(1)], ADD)
-        for cols in quarters:
-            term(D - 1, cols, last_term0[:, cols])
-        nc.vector.tensor_tensor(result, first_three[:], last_term1, ADD)
-        nc.scalar.dma_start(out[:, half(1)], result)
-        for cols in quarters:
-            nc.vector.tensor_tensor(turned_sum[:, cols], turned_back[:, cols], last_term0[:, cols], ADD)
-        nc.sync.dma_start(out[:, half(0)], turned_sum[:])
+        fetched = [[sbuf(f"fetched{d}_{h}", [N, HALF], F32) for h in range(2)] for d in range(D)]
+        turned = [psum.tile([HALF, N], F32, name=f"turned{d}") for d in range(2)]
+        scaled = [sbuf(f"scaled{d}", [HALF, N], F32) for d in range(2)]
+        turned_back = psum.tile([N, HALF], F32, name="turned_back")
+        products = [sbuf(f"product{d}", [N, HALF], F32) for d in range(2)]
+        fused_sums = [sbuf(f"fused_sum{h}", [N, HALF], F32) for h in range(2)]
+        three = sbuf("three", [N, HALF], F32)
+        results = [sbuf(f"result{h}", [N, HALF], F32) for h in range(2)]
+
+        for h in range(2):
+            for d in range(2):
+                nc.scalar.activation(fetched[d][h][:], neighbours(d, h), COPY)
+        for d in range(2):
+            nc.tensor.transpose(turned[d][:], fetched[d][0][:], identity[:])
+        for d in range(2):
+            nc.scalar.activation(scaled[d][:], turned[d][:], COPY, scale=gates_turned[:, d : d + 1])
+            nc.tensor.matmul(turned_back[:], scaled[d][:], identity[:], is_transpose=True, start=d == 0, stop=d == 1)
+        for h in (1, 0):
+            for d in (2, 3):
+                nc.vector.tensor_tensor(fetched[d][h][:], neighbours(d, h), gates_fused[:, d - 2, half(h)], MULT)
+        nc.vector.tensor_tensor(fused_sums[1][:], fetched[2][1][:], fetched[3][1][:], ADD)
+        for d in range(2):
+            nc.vector.tensor_tensor(products[d][:], fetched[d][1][:], gates_after[:, d, :], MULT)
+        nc.vector.tensor_tensor(fused_sums[0][:], fetched[2][0][:], fetched[3][0][:], ADD)
+        nc.vector.tensor_tensor(three[:], fused_sums[1][:], products[0][:], ADD)
+        nc.vector.tensor_tensor(results[1][:], three[:], products[1][:], ADD)
+        nc.scalar.dma_start(out[:, half(1)], results[1][:])
+        nc.vector.tensor_tensor(results[0][:], turned_back[:], fused_sums[0][:], ADD)
+        nc.sync.dma_start(out[:, half(0)], results[0][:])

@@ -52,7 +52,7 @@ def tile_picked_sub_lin_silu_sub_e_kernel(tc, xT, w_words, w_scales, b, gate, of
         x_view = xT.rearrange("(p t) c -> p t c", t=PACK)
         nc.scalar.dma_start(x_planes[0][:], x_view[:, 0, :])
         nc.sync.dma_start(offsets[:], offs)
-        for t in (2, 1, 3):
+        for t in range(1, PACK):
             nc.sync.dma_start(x_planes[t][:], x_view[:, t, :])
         nc.scalar.activation(warm_out[:], warm[:], SILU)
         nc.sync.dma_start(w_codes[:].bitcast(I32), w_words[0].rearrange("p m r -> p (m r)").bitcast(I32))
@@ -66,53 +66,49 @@ def tile_picked_sub_lin_silu_sub_e_kernel(tc, xT, w_words, w_scales, b, gate, of
         nc.sync.dma_start(gates_after[:], gate_rows[:, :2, HALF:])
 
         pieces = S // PIECE
-        last = pieces - 1
-        first_pairs = sbuf("first_pairs", [P, 2, 2, PIECE], U32)
-        other_pairs = sbuf("other_pairs", [P, 1, 2, PIECE], U32)
-
-        def pairs(first, end):
-            return first_pairs[:, first:end, :, :] if first < 2 else other_pairs[:]
-
-        def pair_halves(first, end):
-            return pairs(first, end).bitcast(BF16).rearrange("p i u (c e) -> p i u c e", e=2)
-
+        shared = pieces // 2
+        pairs = [sbuf(f"pairs{i}", [P, 2, PIECE], U32) for i in range(shared)]
+        plain_low = sbuf("plain_low", [P, 2, (pieces - shared) * PIECE], BF16)
+        plain_high = {i: sbuf(f"plain_high{i}", [P, 2, PIECE], BF16) for i in range(shared, pieces)}
         grouped = [sbuf(f"grouped{i}", [P, PIECE, PACK], BF16) for i in range(pieces)]
         scales = [sbuf(f"scales{i}", [P, PIECE], U8) for i in range(pieces)]
         sums = [psum.tile([N, PIECE], F32, name=f"sums{i}") for i in range(pieces)]
-        plain = sbuf("plain", [P, 2, 2 * PIECE], BF16)
         y = sbuf("y", [N, S], F32)
 
         def looked_up(t, first, end):
             return x_planes[t][:].indirect(offsets[:, first * PIECE // LINE : end * PIECE // LINE])
 
-        def gather_to_pairs(t, first, end):
-            nc.vector.tensor_copy(pair_halves(first, end)[:, :, t // 2, :, t % 2], looked_up(t, first, end))
+        def gather_to_pairs(t, i):
+            halves = pairs[i][:].bitcast(BF16).rearrange("p u (c e) -> p u c e", e=2)
+            nc.vector.tensor_copy(halves[:, t // 2, :, t % 2], looked_up(t, i, i + 1))
 
-        def gather_in_place(t):
-            nc.vector.tensor_copy(grouped[last][:, :, t], looked_up(t, last, pieces))
+        def place(i, u, source):
+            nc.vector.tensor_copy(grouped[i][:, :, 2 * u : 2 * u + 2], source.rearrange("p e c -> p c e"))
 
-        gather_to_pairs(0, 0, 2)
-        nc.scalar.activation(plain[:, 0, :], looked_up(0, 2, pieces), COPY)
-        gather_to_pairs(2, 0, 2)
-        gather_to_pairs(2, 2, last)
-        gather_in_place(2)
-        gather_to_pairs(1, 0, 2)
-        nc.scalar.activation(plain[:, 1, :], looked_up(1, 2, pieces), COPY)
-        nc.scalar.copy(pair_halves(2, last)[:, 0, 0, :, :], plain[:, :, :PIECE].rearrange("p e c -> p c e"))
-        nc.scalar.copy(grouped[last][:, :, :2], plain[:, :, PIECE:].rearrange("p e c -> p c e"))
+        for t in range(2):
+            for i in range(shared):
+                gather_to_pairs(t, i)
+            nc.scalar.activation(plain_low[:, t, :], looked_up(t, shared, pieces), COPY)
+        for i in range(shared, pieces):
+            place(i, 0, plain_low[:, :, (i - shared) * PIECE : (i - shared + 1) * PIECE])
+        for t in range(2, PACK):
+            for i in range(shared):
+                gather_to_pairs(t, i)
+            for i in range(shared, pieces):
+                nc.scalar.activation(plain_high[i][:, t - 2, :], looked_up(t, i, i + 1), COPY)
+        for i in range(shared):
+            nc.scalar.copy(grouped[i][:].bitcast(U32), pairs[i][:].rearrange("p u c -> p c u"))
+        for i in range(shared, pieces):
+            place(i, 1, plain_high[i][:])
         columns = sbuf("columns", [P, 16], F32, tag="x_plane0")
         bias = columns[:, 0:1]
         gates_turned = columns[:, 8:10]
         nc.gpsimd.dma_start(bias, b)
         with nc.allow_non_contiguous_dma(reason="one value of gate to a partition"):
             nc.gpsimd.dma_start(gates_turned, gate[:2, 0, :HALF].rearrange("d v -> v d"))
-        for i in range(last):
-            gather_to_pairs(3, i, i + 1)
-            nc.scalar.copy(grouped[i][:].bitcast(U32), pairs(i, i + 1).rearrange("p i u c -> p (i c) u"))
-        gather_in_place(3)
 
-        for i in (0, 1, last, 2):
-            codes = sbuf(f"codes{i}", [P, PIECE], U32, tag="first_pairs" if i == last else None)
+        for i in (2, 0, 3, 1):
+            codes = sbuf(f"codes{i}", [P, PIECE], U32)
             nc.vector.quantize_mx(out=codes[:].bitcast(FP8X4), scales=scales[i][:], in_=grouped[i][:].rearrange("p c t -> p (c t)"))
             nc.tensor.matmul_mx(
                 out=sums[i][:],

@@ -88,7 +88,10 @@ def tile_picked_sub_lin_silu_sub_e_kernel(tc, xT, w_words, w_scales, b, gate, of
         for t in range(2):
             for i in range(shared):
                 gather_to_pairs(t, i)
-            nc.scalar.activation(plain_low[:, t, :], looked_up(t, shared, pieces), COPY)
+            if t == 0:
+                nc.scalar.activation(plain_low[:, t, :], looked_up(t, shared, pieces), COPY)
+        for i in range(shared, pieces):
+            nc.scalar.activation(plain_low[:, 1, (i - shared) * PIECE : (i - shared + 1) * PIECE], looked_up(1, i, i + 1), COPY)
         for i in range(shared, pieces):
             place(i, 0, plain_low[:, :, (i - shared) * PIECE : (i - shared + 1) * PIECE])
         for t in range(2, PACK):

from contextlib import ExitStack

import concourse.mybir as mybir
from concourse.masks import make_identity

K, T, D, S, V, N = 512, 1024, 4, 512, 256, 128
P = 128
PACK = 4
LINE = 16
QUADRANT = 32
PIECE = 128
HALF = V // 2

FLOPS = 2 * K * S * N

F32 = mybir.dt.float32
BF16 = mybir.dt.bfloat16
I32 = mybir.dt.int32
U32 = mybir.dt.uint32
U16 = mybir.dt.uint16
U8 = mybir.dt.uint8
FP8X4 = mybir.dt.float8_e4m3fn_x4
COPY = mybir.ActivationFunctionType.Copy
SILU = mybir.ActivationFunctionType.Silu
MULT = mybir.AluOpType.mult
ADD = mybir.AluOpType.add


def tile_picked_sub_lin_silu_sub_e_kernel(tc, xT, w_words, w_scales, b, gate, offs, pos1, pos2, pos3, pos4, out):
    nc = tc.nc
    with ExitStack() as ctx:
        keep = ctx.enter_context(tc.tile_pool(name="keep", bufs=1))
        psum = ctx.enter_context(tc.psum_pool(name="psum", bufs=1))

        def sbuf(name, shape, dtype, tag=None):
            return keep.tile(shape, dtype, name=name, tag=tag or name, align_bytes=64)

        offsets = keep.tile([P, S // LINE], U16, name="offsets")
        places = [keep.tile([P, V // LINE], U16, name=f"places{d}") for d in range(D)]
        x_planes = [sbuf(f"x_plane{t}", [P, T], F32) for t in range(PACK)]
        w_codes = sbuf("w_codes", [P, N], U32)
        w_scale = sbuf("w_scale", [P, N], U8)
        gates_fused = sbuf("gates_fused", [P, 2, V], F32)
        gates_after = sbuf("gates_after", [P, 2, HALF], F32)
        identity = sbuf("identity", [P, P], F32)
        warm = sbuf("warm", [P, 1], F32)
        warm_out = sbuf("warm_out", [P, 1], F32)

        nc.vector.memset(warm[:], 0.0)
        nc.vector.memset(identity[:], 0.0)
        make_identity(nc, identity[:], nomemset=True)
        x_view = xT.rearrange("(p t) c -> p t c", t=PACK)
        nc.scalar.dma_start(x_planes[0][:], x_view[:, 0, :])
        nc.sync.dma_start(offsets[:], offs)
        for t in range(1, PACK):
            nc.sync.dma_start(x_planes[t][:], x_view[:, t, :])
        nc.scalar.activation(warm_out[:], warm[:], SILU)
        nc.sync.dma_start(w_codes[:].bitcast(I32), w_words[0].rearrange("p m r -> p (m r)").bitcast(I32))
        for q in range(P // QUADRANT):
            rows = w_scale[QUADRANT * q : QUADRANT * q + 4, :]
            (nc.gpsimd if q % 2 else nc.sync).dma_start(rows.bitcast(I32), w_scales[0, 4 * q : 4 * q + 4, :].bitcast(I32))
        gate_rows = gate.rearrange("d m v -> m d v")
        nc.sync.dma_start(gates_fused[:], gate_rows[:, 2:, :])
        for d, pos in ((0, pos1), (2, pos3), (1, pos2), (3, pos4)):
            nc.sync.dma_start(places[d][:], pos)
        nc.sync.dma_start(gates_after[:], gate_rows[:, :2, HALF:])

        pieces = S // PIECE
        shared = pieces // 2
        pairs = [sbuf(f"pairs{i}", [P, 2, PIECE], U32) for i in range(shared)]
        plain_low = sbuf("plain_low", [P, 2, (pieces - shared) * PIECE], BF16)
        plain_high = {i: sbuf(f"plain_high{i}", [P, 2, PIECE], BF16) for i in range(shared, pieces)}
        grouped = [sbuf(f"grouped{i}", [P, PIECE, PACK], BF16) for i in range(pieces)]
        scales = [sbuf(f"scales{i}", [P, PIECE], U8) for i in range(pieces)]
        sums = [psum.tile([N, PIECE], F32, name=f"sums{i}") for i in range(pieces)]
        y = sbuf("y", [N, S], F32)

        def looked_up(t, first, end):
            return x_planes[t][:].indirect(offsets[:, first * PIECE // LINE : end * PIECE // LINE])

        def gather_to_pairs(t, i):
            halves = pairs[i][:].bitcast(BF16).rearrange("p u (c e) -> p u c e", e=2)
            nc.vector.tensor_copy(halves[:, t // 2, :, t % 2], looked_up(t, i, i + 1))

        def place(i, u, source):
            nc.vector.tensor_copy(grouped[i][:, :, 2 * u : 2 * u + 2], source.rearrange("p e c -> p c e"))

        for t in range(2):
            for i in range(shared):
                gather_to_pairs(t, i)
            if t == 0:
                nc.scalar.activation(plain_low[:, t, :], looked_up(t, shared, pieces), COPY)
        for i in range(shared, pieces):
            nc.scalar.activation(plain_low[:, 1, (i - shared) * PIECE : (i - shared + 1) * PIECE], looked_up(1, i, i + 1), COPY)
        for i in range(shared, pieces):
            place(i, 0, plain_low[:, :, (i - shared) * PIECE : (i - shared + 1) * PIECE])
        for t in range(2, PACK):
            for i in range(shared):
                gather_to_pairs(t, i)
            for i in range(shared, pieces):
                nc.scalar.activation(plain_high[i][:, t - 2, :], looked_up(t, i, i + 1), COPY)
        for i in range(shared):
            nc.scalar.copy(grouped[i][:].bitcast(U32), pairs[i][:].rearrange("p u c -> p c u"))
        for i in range(shared, pieces):
            place(i, 1, plain_high[i][:])
        columns = sbuf("columns", [P, 16], F32, tag="x_plane0")
        bias = columns[:, 0:1]
        gates_turned = columns[:, 8:10]
        nc.gpsimd.dma_start(bias, b)
        with nc.allow_non_contiguous_dma(reason="one value of gate to a partition"):
            nc.gpsimd.dma_start(gates_turned, gate[:2, 0, :HALF].rearrange("d v -> v d"))

        for i in (2, 0, 3, 1):
            codes = sbuf(f"codes{i}", [P, PIECE], U32)
            nc.vector.quantize_mx(out=codes[:].bitcast(FP8X4), scales=scales[i][:], in_=grouped[i][:].rearrange("p c t -> p (c t)"))
            nc.tensor.matmul_mx(
                out=sums[i][:],
                lhsT=w_codes[:].bitcast(FP8X4),
                lhsT_scale=w_scale[:],
                rhs=codes[:].bitcast(FP8X4),
                rhs_scale=scales[i][:],
                start=True,
                stop=True,
            )
            nc.scalar.activation(y[:, i * PIECE : (i + 1) * PIECE], sums[i][:], SILU, bias=bias)

        def half(h):
            return slice(h * HALF, (h + 1) * HALF)

        def neighbours(d, h):
            return y[:].indirect(places[d][:, h * HALF // LINE : (h + 1) * HALF // LINE])

        fetched = [[sbuf(f"fetched{d}_{h}", [N, HALF], F32) for h in range(2)] for d in range(D)]
        turned = [psum.tile([HALF, N], F32, name=f"turned{d}") for d in range(2)]
        scaled = [sbuf(f"scaled{d}", [HALF, N], F32) for d in range(2)]
        turned_back = psum.tile([N, HALF], F32, name="turned_back")
        products = [sbuf(f"product{d}", [N, HALF], F32) for d in range(2)]
        fused_sums = [sbuf(f"fused_sum{h}", [N, HALF], F32) for h in range(2)]
        three = sbuf("three", [N, HALF], F32)
        results = [sbuf(f"result{h}", [N, HALF], F32) for h in range(2)]

        for h in range(2):
            for d in range(2):
                nc.scalar.activation(fetched[d][h][:], neighbours(d, h), COPY)
        for d in range(2):
            nc.tensor.transpose(turned[d][:], fetched[d][0][:], identity[:])
        for d in range(2):
            nc.scalar.activation(scaled[d][:], turned[d][:], COPY, scale=gates_turned[:, d : d + 1])
            nc.tensor.matmul(turned_back[:], scaled[d][:], identity[:], is_transpose=True, start=d == 0, stop=d == 1)
        for h in (1, 0):
            for d in (2, 3):
                nc.vector.tensor_tensor(fetched[d][h][:], neighbours(d, h), gates_fused[:, d - 2, half(h)], MULT)
        nc.vector.tensor_tensor(fused_sums[1][:], fetched[2][1][:], fetched[3][1][:], ADD)
        for d in range(2):
            nc.vector.tensor_tensor(products[d][:], fetched[d][1][:], gates_after[:, d, :], MULT)
        nc.vector.tensor_tensor(fused_sums[0][:], fetched[2][0][:], fetched[3][0][:], ADD)
        nc.vector.tensor_tensor(three[:], fused_sums[1][:], products[0][:], ADD)
        nc.vector.tensor_tensor(results[1][:], three[:], products[1][:], ADD)
        nc.scalar.dma_start(out[:, half(1)], results[1][:])
        nc.vector.tensor_tensor(results[0][:], turned_back[:], fused_sums[0][:], ADD)
        nc.sync.dma_start(out[:, half(0)], results[0][:])
